import numpy as np
import ml_dtypes


def mxq(x, axis, fmt="e4m3"):
    dtype, down = {"e4m3": (ml_dtypes.float8_e4m3fn, 7), "e5m2": (ml_dtypes.float8_e5m2, 14)}[fmt]
    v = np.moveaxis(np.asarray(x, np.float32).astype(ml_dtypes.bfloat16).astype(np.float64), axis, -1)
    blocks = v.reshape(v.shape[:-1] + (-1, 32))
    amax = np.abs(blocks).max(-1, keepdims=True)
    byte = np.maximum(np.where(amax > 0, np.frexp(amax)[1] - 1 + 127, 0) - down, 1)
    scale = np.exp2(byte - 127.0)
    codes = (blocks / scale).astype(np.float32).astype(dtype).astype(np.float64)
    return np.moveaxis((codes * scale).reshape(v.shape), -1, axis)


WIDE = False


def mx_kscale(k):
    if not WIDE:
        return np.ones(k)
    levels = np.array([10, -10, 5, -5, 0])
    if k % 512:
        return np.exp2(np.random.permutation(np.resize(levels, k // 32))).repeat(32)
    a = np.empty((k // 512, 16))
    for p in range(k // 512):
        a[p, :8] = np.random.permutation(np.resize(levels, 8))
        for g in range(8):
            far = levels[np.abs(levels - a[p, g]) >= 10]
            a[p, g + 8] = far[np.random.randint(len(far))]
    return np.exp2(a.ravel()).repeat(32)


def f64(x):
    return np.asarray(x).astype(np.float64)


def striped(idx):
    return np.tile(idx.reshape(-1, 16).T, (8, 1)).astype(np.uint16)


def unstriped(offs):
    return offs[:16].T.reshape(-1).astype(np.int64)


E2M1 = np.array([0.0, 0.5, 1.0, 1.5, 2.0, 3.0, 4.0, 6.0, -0.0, -0.5, -1.0, -1.5, -2.0, -3.0, -4.0, -6.0])


def pack_weight(w, fmt):
    k, n = w.shape
    w = f64(np.asarray(w, np.float32).astype(ml_dtypes.bfloat16)).reshape(k // 32, 32, n)
    amax = np.abs(w).max(1)
    if fmt == "e4m3":
        byte = np.frexp(amax)[1] - 1 + 127 - 7
    else:
        mant, ex = np.frexp(amax / 6.0)
        byte = np.where(mant > 0.5, ex, ex - 1) + 127
    byte = np.clip(np.where(amax > 0, byte, 1), 1, 254)
    scaled = (w * np.exp2(127.0 - byte)[:, None, :]).reshape(k, n).astype(np.float32)
    by_word = np.ascontiguousarray(scaled.reshape(k // 512, 128, 4, n).transpose(0, 1, 3, 2))
    if fmt == "e4m3":
        words = by_word.astype(ml_dtypes.float8_e4m3fn).view(np.uint8)
    else:
        c = by_word.astype(ml_dtypes.float4_e2m1fn).view(np.uint8) & 0xF
        words = (c[..., 0::2] | (c[..., 1::2] << 4)).reshape(k // 512, 128, 2 * n)
    return np.ascontiguousarray(words), np.ascontiguousarray(byte.astype(np.uint8).reshape(k // 512, 16, n))


def unpack_weight(words, scales, fmt):
    g, _, n = scales.shape
    words = np.ascontiguousarray(words).reshape(g, 128, n, -1)
    if fmt == "e4m3":
        vals = words.view(ml_dtypes.float8_e4m3fn).astype(np.float64)
    else:
        nib = np.empty((g, 128, n, 4), np.uint8)
        nib[..., 0::2] = words & 0xF
        nib[..., 1::2] = words >> 4
        vals = E2M1[nib]
    vals = vals * np.repeat(np.exp2(scales.astype(np.float64) - 127.0), 8, axis=1)[..., None]
    return vals.transpose(0, 1, 3, 2).reshape(g * 512, n)


def gelu(v):
    return 0.5 * v * (1.0 + np.tanh(np.sqrt(2.0 / np.pi) * (v + 0.044715 * v**3)))


def striped8(idx):
    return np.concatenate([v.reshape(-1, 16).T for v in idx]).astype(np.uint16)


def unstriped8(offs):
    return np.stack([offs[16 * g:16 * g + 16].T.reshape(-1) for g in range(8)]).astype(np.int64)


def heads(h, wgt, idx8):
    r = np.arange(h.shape[0])
    return wgt[r // 4 % 128] * h[r[:, None], idx8[r % 512 // 64]]


def put_heads(h, wgs, idx8, t2):
    r = np.arange(h.shape[0])
    page = np.zeros((h.shape[0], t2))
    page[r[:, None], idx8[r % 512 // 64]] = wgs[r // 4 % 128] * h
    return page


K, T, S, H, T2, P, N = 512, 4096, 1024, 1024, 2048, 1024, 512


def setup_inputs():
    n = np.random.standard_normal
    s = mx_kscale(K)[:, None]
    u = mx_kscale(H)[:, None]
    d = {}
    d["tab_words"], d["tab_scales"] = pack_weight(n((K, T)) * s, "e4m3")
    d["offs"] = striped(np.random.permutation(T)[:S])
    d["offs2"] = striped8(np.stack([np.random.permutation(T2)[:S] for _ in range(8)]))
    d["offs3"] = striped8(np.stack([np.random.permutation(T2)[:P] for _ in range(8)]))
    d["w1"] = (n((K, H)) / s / K ** 0.5).astype(np.float32)
    d["w2_words"], d["w2_scales"] = pack_weight(n((K, H)) / s / K ** 0.5, "e2m1")
    d["b1"] = (0.6 * n(H)).astype(np.float32)
    d["wgs"] = np.repeat(np.random.uniform(0.5, 2.0, (8, S)), 16, axis=0).astype(np.float32)
    d["wgt"] = np.repeat(np.random.uniform(0.5, 2.0, (8, P)), 16, axis=0).astype(np.float32)
    d["vac"] = (n((H, P)) * u).astype(np.float32)
    d["w3"] = (1.3 * n((H, N)) / u / H ** 0.5).astype(np.float32)
    d["b3"] = (0.5 * n(N)).astype(np.float32)
    return d


def reference(tab_words, tab_scales, offs, offs2, offs3, w1, w2_words, w2_scales, b1, wgs, wgt, vac, w3, b3):
    v = unpack_weight(tab_words, tab_scales, "e4m3")[:, unstriped(offs)]
    flow = mxq(f64(w1), 0, "e4m3").T @ v
    valve = unpack_weight(w2_words, w2_scales, "e2m1").T @ v
    h = flow * valve + f64(b1)[:, None]
    page = put_heads(h, f64(wgs), unstriped8(offs2), T2)
    x = heads(page, f64(wgt), unstriped8(offs3))
    z = f64(vac) / (1.0 + np.square(x))
    out = mxq(f64(w3), 0, "e4m3").T @ mxq(z, 0, "e4m3")
    return out + f64(b3)[:, None]

@@ -1,0 +1,248 @@
+import math
+from contextlib import ExitStack
+
+import concourse.mybir as mybir
+
+K, T, S, H, T2, M, N = 512, 4096, 1024, 1024, 2048, 1024, 512
+FLOPS = 2 * (2 * K * H * S + H * N * M)
+
+F32 = mybir.dt.float32
+BF16 = mybir.dt.bfloat16
+I32 = mybir.dt.int32
+U32 = mybir.dt.uint32
+U16 = mybir.dt.uint16
+U8 = mybir.dt.uint8
+FP8X4 = mybir.dt.float8_e4m3fn_x4
+FP4X4 = mybir.dt.float4_e2m1fn_x4
+ACT = mybir.ActivationFunctionType
+MULT = mybir.AluOpType.mult
+
+P = 128
+PACK = 4
+PASS = P * PACK
+BANK = 512
+BLOCKS = H // PASS
+SLICES = BLOCKS * PACK
+CHUNKS = [(0, 256), (256, 256), (512, 256), (768, 128), (896, 128)]
+ROOT_SHIFT = 1.125
+
+
+def tile_list_well_vacuum_scores_kernel(
+    tc, tab_words, tab_scales, offs, offs2, offs3, w1, w2_words, w2_scales, b1, wgs, wgt, vac, w3, b3, out
+):
+    nc = tc.nc
+    with ExitStack() as ctx:
+        keep = ctx.enter_context(tc.tile_pool(name="keep", bufs=1))
+        ring = ctx.enter_context(tc.tile_pool(name="ring", bufs=2))
+        psum = ctx.enter_context(tc.psum_pool(name="psum", bufs=1))
+
+        idx1 = keep.tile([P, S // 16], U16, name="idx1")
+        idx2 = keep.tile([P, S // 16], U16, name="idx2")
+        idx3 = keep.tile([P, M // 16], U16, name="idx3")
+        tab_w = keep.tile([P, T], I32, name="tab_w", tag="tab_then_vac", align_bytes=64)
+        tab_s = keep.tile([P, T], U8, name="tab_s", tag="scales_then_codes", align_bytes=64)
+        w2_raw = keep.tile([P, 2 * H], U8, name="w2_raw", tag="raw_weights", align_bytes=64)
+        w2_raw_s = keep.tile([P, H], U8, name="w2_raw_s", tag="scales_then_wgs", align_bytes=64)
+        b1_sb = keep.tile([P, BLOCKS, PACK], F32, name="b1_sb")
+        b3_sb = keep.tile([P, PACK], F32, name="b3_sb")
+        pages = [keep.tile([P, T2], F32, name=f"page{i}") for i in range(2)]
+
+        nc.vector.memset(tab_s[:].bitcast(I32), 0)
+        nc.vector.memset(w2_raw_s[:].bitcast(I32), 0)
+        for page in pages:
+            nc.vector.memset(page[:], 0.0)
+
+        def load_rows(rows):
+            raw = keep.tile([P, 2, PACK, PASS // 2], F32, name="w_raw", tag="raw_weights", align_bytes=64)
+            for half in range(2):
+                cols = slice(half * PASS // 2, (half + 1) * PASS // 2)
+                nc.sync.dma_start(raw[:, half], rows[:, cols].rearrange("(p j) c -> p j c", j=PACK))
+            return raw
+
+        def load_vac(b):
+            v = keep.tile([P, PACK, M], F32, name=f"vac{b}", tag="tab_then_vac", align_bytes=64)
+            nc.sync.dma_start(v[:], vac[b * PASS : (b + 1) * PASS, :].rearrange("(p j) m -> p j m", j=PACK))
+            return v
+
+        nc.sync.dma_start(idx1[:], offs)
+        nc.sync.dma_start(w2_raw[:].bitcast(I32), w2_words[0].bitcast(I32))
+        nc.sync.dma_start(idx2[:], offs2)
+        nc.sync.dma_start(idx3[:], offs3)
+        nc.sync.dma_start(tab_w[:], tab_words[0].rearrange("p t i -> p (t i)").bitcast(I32))
+        for q in range(4):
+            nc.scalar.dma_start(tab_s[32 * q : 32 * q + 4, :].bitcast(I32), tab_scales[0, 4 * q : 4 * q + 4, :].bitcast(I32))
+        for q in range(4):
+            nc.scalar.dma_start(
+                w2_raw_s[32 * q : 32 * q + 4, :].bitcast(I32), w2_scales[0, 4 * q : 4 * q + 4, :].bitcast(I32)
+            )
+        nc.gpsimd.dma_start(b1_sb[:], b1.rearrange("(b p t) -> p b t", p=P, t=PACK))
+        nc.gpsimd.dma_start(b3_sb[:], b3.rearrange("(p t) -> p t", t=PACK))
+
+        w2_codes = keep.tile([P, 2 * H], U8, name="w2_codes", align_bytes=64)
+        w2_s = keep.tile([P, H], U8, name="w2_s", align_bytes=64)
+        w1_codes = keep.tile([P, H], U32, name="w1_codes", align_bytes=64)
+        w1_s = keep.tile([P, H], U8, name="w1_s", align_bytes=64)
+        w3_codes = keep.tile([P, BLOCKS * N], U32, name="w3_codes", align_bytes=64)
+        w3_s = keep.tile([P, BLOCKS * N], U8, name="w3_s", align_bytes=64)
+
+        def quantize_weight_pair(raw, pair, codes, scales, col0, grouped=None):
+            if grouped is None:
+                grouped = ring.tile([P, 2 * PASS], BF16, name="w_grouped", align_bytes=64)
+            for half in range(2):
+                nc.scalar.copy(
+                    grouped[:].rearrange("p (t h m j) -> p h m j t", t=2, h=2, j=PACK)[:, half],
+                    raw[:, half].rearrange("p j (m t) -> p m j t", t=PACK)[:, :, :, 2 * pair : 2 * pair + 2],
+                )
+            cols = slice(col0 + 2 * P * pair, col0 + 2 * P * (pair + 1))
+            nc.vector.quantize_mx(codes[:, cols].bitcast(FP8X4), scales[:, cols], grouped[:])
+
+        v_s = keep.tile([P, S], U8, name="v_s", align_bytes=64)
+        nc.vector.tensor_copy(
+            w2_codes[:].bitcast(U16).rearrange("p (b t m) -> p b t m", b=BLOCKS, t=PACK),
+            w2_raw[:].bitcast(U16).rearrange("p (b m t) -> p b t m", b=BLOCKS, t=PACK),
+        )
+        w1_raw = load_rows(w1[:, 0:PASS])
+        nc.vector.tensor_copy(v_s[:], tab_s[:].indirect(idx1[:]))
+        v_codes = keep.tile([P, S], U32, name="v_codes", tag="scales_then_codes", align_bytes=64)
+        nc.vector.tensor_copy(v_codes[:], tab_w[:].bitcast(U32).indirect(idx1[:]))
+        nc.vector.tensor_copy(
+            w2_s[:].rearrange("p (b t m) -> p b t m", b=BLOCKS, t=PACK),
+            w2_raw_s[:].rearrange("p (b m t) -> p b t m", b=BLOCKS, t=PACK),
+        )
+        wgs_sb = keep.tile([P, S], F32, name="wgs_sb", tag="scales_then_wgs", align_bytes=64)
+        nc.sync.dma_start(wgs_sb[:], wgs)
+        first = keep.tile([P, 2 * PASS], BF16, name="first", tag="grouped_then_wgt", align_bytes=64)
+        quantize_weight_pair(w1_raw, 0, w1_codes, w1_s, 0, first)
+        wgt_sb = keep.tile([P, M], F32, name="wgt_sb", tag="grouped_then_wgt", align_bytes=64)
+        nc.sync.dma_start(wgt_sb[:], wgt)
+        quantize_weight_pair(w1_raw, 1, w1_codes, w1_s, 0)
+        w1_raw = load_rows(w1[:, PASS : 2 * PASS])
+        vac_sb = [load_vac(0)]
+
+        damp = [keep.tile([P, PACK * M], F32, name=f"damp{b}") for b in range(BLOCKS)]
+        z_codes = [keep.tile([P, M], U32, name=f"z_codes{b}", align_bytes=64) for b in range(BLOCKS)]
+        z_s = [keep.tile([P, M], U8, name=f"z_s{b}", align_bytes=64) for b in range(BLOCKS)]
+        h_tiles = {}
+        x_tiles = {}
+
+        def products(s):
+            cols = slice(s * P, (s + 1) * P)
+            h = ring.tile([P, S], F32, name="h")
+            valve_sb = ring.tile([P, S], F32, name="valve_sb")
+            for half in range(S // BANK):
+                span = slice(half * BANK, (half + 1) * BANK)
+                valve = psum.tile([P, BANK], F32, name=f"bank{4 * (s % 2) + 2 * half}")
+                flow = psum.tile([P, BANK], F32, name=f"bank{4 * (s % 2) + 2 * half + 1}")
+                nc.tensor.matmul_mx(
+                    valve[:], w2_codes[:, 2 * s * P : 2 * (s + 1) * P].bitcast(FP4X4), w2_s[:, cols],
+                    v_codes[:, span].bitcast(FP8X4), v_s[:, span], start=True, stop=True,
+                )
+                nc.tensor.matmul_mx(
+                    flow[:], w1_codes[:, cols].bitcast(FP8X4), w1_s[:, cols],
+                    v_codes[:, span].bitcast(FP8X4), v_s[:, span], start=True, stop=True,
+                )
+                nc.scalar.copy(valve_sb[:, span], valve[:])
+                nc.vector.tensor_tensor(h[:, span], flow[:], valve_sb[:, span], MULT)
+            h_tiles[s] = h
+
+        def put(s):
+            h = h_tiles[s]
+            bias = b1_sb[:, s // PACK, s % PACK : s % PACK + 1]
+            nc.scalar.activation(h[:], h[:], ACT.Identity, bias=bias)
+            nc.vector.tensor_tensor(pages[s % 2][:].indirect(idx2[:]), h[:], wgs_sb[:], MULT)
+
+        def take(s, start, width):
+            span = slice(start, start + width)
+            nc.vector.tensor_tensor(
+                x_tiles[s][:, span], pages[s % 2][:].indirect(idx3[:, start // 16 : (start + width) // 16]),
+                wgt_sb[:, span], MULT,
+            )
+
+        def damping(s, start, width):
+            x = x_tiles[s]
+            span = slice(start, start + width)
+            nc.scalar.activation(x[:, span], x[:, span], ACT.Square)
+            nc.scalar.activation(x[:, span], x[:, span], ACT.Abs_reciprocal_sqrt, bias=ROOT_SHIFT, scale=ROOT_SHIFT)
+            for c0, cw in CHUNKS:
+                if start <= c0 < start + width:
+                    at = PACK * c0 + (s % PACK) * cw
+                    nc.scalar.activation(
+                        damp[s // PACK][:, at : at + cw], x[:, c0 : c0 + cw], ACT.Square, scale=math.sqrt(ROOT_SHIFT)
+                    )
+
+        def quantize_z(b, start, width):
+            z = ring.tile([P, PACK * 256], BF16, name="z", align_bytes=64)
+            nc.vector.tensor_tensor(
+                z[:, 0 : PACK * width].rearrange("p (c i t) -> p c t i", i=2, t=PACK),
+                damp[b][:, PACK * start : PACK * (start + width)].rearrange("p (t c i) -> p c t i", t=PACK, i=2),
+                vac_sb[b][:, :, start : start + width].rearrange("p t (c i) -> p c t i", i=2),
+                MULT,
+            )
+            span = slice(start, start + width)
+            nc.vector.quantize_mx(z_codes[b][:, span].bitcast(FP8X4), z_s[b][:, span], z[:, 0 : PACK * width])
+
+        score_banks = {}
+
+        def scores(b, start, width):
+            per_bank = BANK // width
+            span = slice(start, start + width)
+            for t in range(PACK):
+                bank_no = (PACK * start) // BANK + t // per_bank
+                if bank_no not in score_banks:
+                    score_banks[bank_no] = psum.tile([P, BANK], F32, name=f"bank{bank_no}")
+                at = (t % per_bank) * width
+                cols = slice(b * N + t * P, b * N + (t + 1) * P)
+                nc.tensor.matmul_mx(
+                    score_banks[bank_no][:, at : at + width], w3_codes[:, cols].bitcast(FP8X4), w3_s[:, cols],
+                    z_codes[b][:, span].bitcast(FP8X4), z_s[b][:, span],
+                    start=(b == 0 and t % per_bank == 0), stop=(b == BLOCKS - 1 and t % per_bank == per_bank - 1),
+                )
+
+        out_rows = out.rearrange("(p t) m -> p t m", t=PACK)
+
+        def store(start, width):
+            per_bank = BANK // width
+            staged = keep.tile([P, PACK, width], F32, name=f"staged{start}")
+            for t in range(PACK):
+                bank_no = (PACK * start) // BANK + t // per_bank
+                at = (t % per_bank) * width
+                nc.scalar.activation(
+                    staged[:, t, :], score_banks[bank_no][:, at : at + width], ACT.Identity, bias=b3_sb[:, t : t + 1]
+                )
+            nc.sync.dma_start(out_rows[:, :, start : start + width], staged[:])
+
+        last = SLICES - 1
+        products(0)
+        products(1)
+        put(0)
+        for s in range(SLICES):
+            x_tiles[s] = ring.tile([P, M], F32, name="x")
+            if s < last:
+                take(s, 0, M)
+            if s + 2 <= last:
+                products(s + 2)
+            if s + 1 <= last:
+                put(s + 1)
+            if s < last:
+                damping(s, 0, M)
+            if s == 0:
+                for pair in range(2):
+                    quantize_weight_pair(w1_raw, pair, w1_codes, w1_s, PASS)
+            if s in (2, 4):
+                b = s // 2 - 1
+                w3_raw = load_rows(w3[b * PASS : (b + 1) * PASS, :])
+                for pair in range(2):
+                    quantize_weight_pair(w3_raw, pair, w3_codes, w3_s, b * N)
+            if s == PACK - 1:
+                for start, width in CHUNKS:
+                    quantize_z(0, start, width)
+                vac_sb.append(load_vac(1))
+        for start, width in CHUNKS:
+            scores(0, start, width)
+        for start, width in CHUNKS:
+            take(last, start, width)
+            damping(last, start, width)
+        for start, width in CHUNKS:
+            quantize_z(1, start, width)
+            scores(1, start, width)
+            store(start, width)

@@ -16,6 +16,7 @@ FP8X4 = mybir.dt.float8_e4m3fn_x4
 FP4X4 = mybir.dt.float4_e2m1fn_x4
 ACT = mybir.ActivationFunctionType
 MULT = mybir.AluOpType.mult
+ADD = mybir.AluOpType.add
 
 P = 128
 PACK = 4
@@ -60,7 +61,7 @@ def tile_list_well_vacuum_scores_kernel(
             return raw
 
         def load_vac(b):
-            v = keep.tile([P, PACK, M], F32, name=f"vac{b}", tag="tab_then_vac", align_bytes=64)
+            v = keep.tile([P, PACK, M], F32, name=f"vac{b}", tag=("tab_then_vac", "raw_weights")[b], align_bytes=64)
             nc.sync.dma_start(v[:], vac[b * PASS : (b + 1) * PASS, :].rearrange("(p j) m -> p j m", j=PACK))
             return v
 
@@ -96,6 +97,17 @@ def tile_list_well_vacuum_scores_kernel(
             cols = slice(col0 + 2 * P * pair, col0 + 2 * P * (pair + 1))
             nc.vector.quantize_mx(codes[:, cols].bitcast(FP8X4), scales[:, cols], grouped[:])
 
+        def quantize_weight_block(raw, codes, scales, col0):
+            grouped = ring.tile([P, PACK * PASS], BF16, name="w_grouped", align_bytes=64)
+            for pair in range(2):
+                for half in range(2):
+                    nc.scalar.copy(
+                        grouped[:].rearrange("p (u t h m j) -> p u h m j t", u=2, t=2, h=2, j=PACK)[:, pair, half],
+                        raw[:, half].rearrange("p j (m t) -> p m j t", t=PACK)[:, :, :, 2 * pair : 2 * pair + 2],
+                    )
+            cols = slice(col0, col0 + PASS)
+            nc.vector.quantize_mx(codes[:, cols].bitcast(FP8X4), scales[:, cols], grouped[:])
+
         v_s = keep.tile([P, S], U8, name="v_s", align_bytes=64)
         nc.vector.tensor_copy(
             w2_codes[:].bitcast(U16).rearrange("p (b t m) -> p b t m", b=BLOCKS, t=PACK),
@@ -125,10 +137,14 @@ def tile_list_well_vacuum_scores_kernel(
         h_tiles = {}
         x_tiles = {}
 
+        last = SLICES - 1
+        work = {-2: ring.tile([P, 2, S], F32, name="work", bufs=3)}
+
         def products(s):
             cols = slice(s * P, (s + 1) * P)
-            h = ring.tile([P, S], F32, name="h")
-            valve_sb = ring.tile([P, S], F32, name="valve_sb")
+            work[s - 1] = ring.tile([P, 2, S], F32, name="work", bufs=3)
+            h = work[s - 1][:, 0, :]
+            valve_sb = work[s - 2][:, 1, :]
             for half in range(S // BANK):
                 span = slice(half * BANK, (half + 1) * BANK)
                 valve = psum.tile([P, BANK], F32, name=f"bank{4 * (s % 2) + 2 * half}")
@@ -142,33 +158,81 @@ def tile_list_well_vacuum_scores_kernel(
                     v_codes[:, span].bitcast(FP8X4), v_s[:, span], start=True, stop=True,
                 )
                 nc.scalar.copy(valve_sb[:, span], valve[:])
-                nc.vector.tensor_tensor(h[:, span], flow[:], valve_sb[:, span], MULT)
+                if s == 0:
+                    nc.vector.tensor_tensor(h[:, span], flow[:], valve_sb[:, span], MULT)
+                else:
+                    nc.scalar.copy(h[:, span], flow[:])
+            if s > 0:
+                nc.gpsimd.tensor_tensor(h, h, valve_sb, MULT)
             h_tiles[s] = h
 
-        def put(s):
+        def weigh(s):
             h = h_tiles[s]
             bias = b1_sb[:, s // PACK, s % PACK : s % PACK + 1]
-            nc.scalar.activation(h[:], h[:], ACT.Identity, bias=bias)
-            nc.vector.tensor_tensor(pages[s % 2][:].indirect(idx2[:]), h[:], wgs_sb[:], MULT)
+            if s == 0:
+                for half in range(S // BANK):
+                    span = slice(half * BANK, (half + 1) * BANK)
+                    nc.vector.scalar_tensor_tensor(h[:, span], h[:, span], bias, wgs_sb[:, span], ADD, MULT)
+            else:
+                nc.scalar.activation(h, h, ACT.Identity, bias=bias)
+                placed = ring.tile([P, S], F32, name="placed")
+                nc.gpsimd.tensor_tensor(placed[:], h, wgs_sb[:], MULT)
+                h_tiles[s] = placed[:]
 
-        def take(s, start, width):
+        def put(s):
+            nc.vector.tensor_copy(pages[s % 2][:].indirect(idx2[:]), h_tiles[s])
+
+        def take(s):
+            x_tiles[s] = ring.tile([P, M], F32, name="x")
+            nc.vector.tensor_copy(x_tiles[s][:], pages[s % 2][:].indirect(idx3[:]))
+
+        def take_weighed(s, start, width):
             span = slice(start, start + width)
             nc.vector.tensor_tensor(
                 x_tiles[s][:, span], pages[s % 2][:].indirect(idx3[:, start // 16 : (start + width) // 16]),
                 wgt_sb[:, span], MULT,
             )
 
-        def damping(s, start, width):
-            x = x_tiles[s]
-            span = slice(start, start + width)
-            nc.scalar.activation(x[:, span], x[:, span], ACT.Square)
-            nc.scalar.activation(x[:, span], x[:, span], ACT.Abs_reciprocal_sqrt, bias=ROOT_SHIFT, scale=ROOT_SHIFT)
-            for c0, cw in CHUNKS:
-                if start <= c0 < start + width:
-                    at = PACK * c0 + (s % PACK) * cw
-                    nc.scalar.activation(
-                        damp[s // PACK][:, at : at + cw], x[:, c0 : c0 + cw], ACT.Square, scale=math.sqrt(ROOT_SHIFT)
-                    )
+        def damping(s, x, pieces):
+            nc.scalar.activation(x, x, ACT.Square)
+            nc.scalar.activation(x, x, ACT.Abs_reciprocal_sqrt, bias=ROOT_SHIFT, scale=ROOT_SHIFT)
+            for dst, src in pieces:
+                nc.scalar.activation(dst, src, ACT.Square, scale=math.sqrt(ROOT_SHIFT))
+
+        def damp_piece(s, start, width):
+            at = PACK * start + (s % PACK) * width
+            return damp[s // PACK][:, at : at + width]
+
+        def weigh_taken(s):
+            x = work[s][:, :, 0:BANK]
+            nc.gpsimd.tensor_tensor(
+                x, x_tiles[s][:].rearrange("p (h c) -> p h c", h=2), wgt_sb[:].rearrange("p (h c) -> p h c", h=2), MULT
+            )
+
+        def damp_taken(s):
+            x = work[s][:, :, 0:BANK]
+            if s < PACK:
+                pieces = [(damp_piece(s, 0, M).rearrange("p (h c) -> p h c", h=2), x)]
+            else:
+                pieces = [
+                    (damp_piece(s, c0, cw), work[s][:, c0 // BANK, c0 % BANK : c0 % BANK + cw]) for c0, cw in CHUNKS
+                ]
+            damping(s, x, pieces)
+
+        z_rows = keep.tile([P, PACK, M], BF16, name="z_rows", align_bytes=64)
+
+        def first_z_row(t):
+            nc.gpsimd.tensor_tensor(z_rows[:, t, :], damp[0][:, t * M : (t + 1) * M], vac_sb[0][:, t, :], MULT)
+
+        def quantize_first_z():
+            for half in range(2):
+                span = slice(half * BANK, (half + 1) * BANK)
+                z = ring.tile([P, PACK * BANK], BF16, name="w_grouped", align_bytes=64)
+                nc.scalar.copy(
+                    z[:].rearrange("p (c i t) -> p c t i", i=4, t=PACK),
+                    z_rows[:, :, span].rearrange("p t (c i) -> p c t i", i=4),
+                )
+                nc.vector.quantize_mx(z_codes[0][:, span].bitcast(FP8X4), z_s[0][:, span], z[:])
 
         def quantize_z(b, start, width):
             z = ring.tile([P, PACK * 256], BF16, name="z", align_bytes=64)
@@ -211,37 +275,40 @@ def tile_list_well_vacuum_scores_kernel(
                 )
             nc.sync.dma_start(out_rows[:, :, start : start + width], staged[:])
 
-        last = SLICES - 1
         products(0)
+        weigh(0)
         products(1)
-        put(0)
         for s in range(SLICES):
-            x_tiles[s] = ring.tile([P, M], F32, name="x")
-            if s < last:
-                take(s, 0, M)
+            put(s)
+            if s >= 1:
+                weigh_taken(s - 1)
+            if s + 1 <= last:
+                weigh(s + 1)
             if s + 2 <= last:
                 products(s + 2)
-            if s + 1 <= last:
-                put(s + 1)
+            if s >= 1:
+                damp_taken(s - 1)
             if s < last:
-                damping(s, 0, M)
+                take(s)
             if s == 0:
-                for pair in range(2):
-                    quantize_weight_pair(w1_raw, pair, w1_codes, w1_s, PASS)
-            if s in (2, 4):
-                b = s // 2 - 1
+                quantize_weight_block(w1_raw, w1_codes, w1_s, PASS)
+            if s in (4, 5):
+                first_z_row(s - 4)
+                b = s - 4
                 w3_raw = load_rows(w3[b * PASS : (b + 1) * PASS, :])
-                for pair in range(2):
-                    quantize_weight_pair(w3_raw, pair, w3_codes, w3_s, b * N)
-            if s == PACK - 1:
-                for start, width in CHUNKS:
-                    quantize_z(0, start, width)
+                quantize_weight_block(w3_raw, w3_codes, w3_s, b * N)
+            if s == 6:
+                first_z_row(2)
+                first_z_row(3)
                 vac_sb.append(load_vac(1))
+                quantize_first_z()
         for start, width in CHUNKS:
             scores(0, start, width)
+        x_tiles[last] = ring.tile([P, M], F32, name="x")
         for start, width in CHUNKS:
-            take(last, start, width)
-            damping(last, start, width)
+            take_weighed(last, start, width)
+            x = x_tiles[last][:, start : start + width]
+            damping(last, x, [(damp_piece(last, start, width), x)])
         for start, width in CHUNKS:
             quantize_z(1, start, width)
             scores(1, start, width)

@@ -26,6 +26,9 @@ BLOCKS = H // PASS
 SLICES = BLOCKS * PACK
 CHUNKS = [(0, 256), (256, 256), (512, 256), (768, 128), (896, 128)]
 ROOT_SHIFT = 1.125
+B1_AT = 16384
+W2S_AT = B1_AT + 32
+WGS_AT = W2S_AT + H
 
 
 def tile_list_well_vacuum_scores_kernel(
@@ -35,51 +38,43 @@ def tile_list_well_vacuum_scores_kernel(
     with ExitStack() as ctx:
         keep = ctx.enter_context(tc.tile_pool(name="keep", bufs=1))
         ring = ctx.enter_context(tc.tile_pool(name="ring", bufs=2))
+        head = ctx.enter_context(tc.tile_pool(name="head", bufs=1))
         psum = ctx.enter_context(tc.psum_pool(name="psum", bufs=1))
 
         idx1 = keep.tile([P, S // 16], U16, name="idx1")
         idx2 = keep.tile([P, S // 16], U16, name="idx2")
         idx3 = keep.tile([P, M // 16], U16, name="idx3")
-        tab_w = keep.tile([P, T], I32, name="tab_w", tag="tab_then_vac", align_bytes=64)
+        tab_w = keep.tile([P, T], I32, name="tab_w", tag="table_then_w3", align_bytes=64)
         tab_s = keep.tile([P, T], U8, name="tab_s", tag="scales_then_codes", align_bytes=64)
-        w2_raw = keep.tile([P, 2 * H], U8, name="w2_raw", tag="raw_weights", align_bytes=64)
-        w2_raw_s = keep.tile([P, H], U8, name="w2_raw_s", tag="scales_then_wgs", align_bytes=64)
-        b1_sb = keep.tile([P, BLOCKS, PACK], F32, name="b1_sb")
-        b3_sb = keep.tile([P, PACK], F32, name="b3_sb")
+        w2_raw = head.tile([P, 2 * H], U8, name="w2_raw", offset=B1_AT - 512)
         pages = [keep.tile([P, T2], F32, name=f"page{i}") for i in range(2)]
 
         nc.vector.memset(tab_s[:].bitcast(I32), 0)
-        nc.vector.memset(w2_raw_s[:].bitcast(I32), 0)
-        for page in pages:
-            nc.vector.memset(page[:], 0.0)
+        nc.vector.memset(pages[0][:], 0.0)
 
-        def load_rows(rows):
-            raw = keep.tile([P, 2, PACK, PASS // 2], F32, name="w_raw", tag="raw_weights", align_bytes=64)
+        warm = keep.tile([P, 2], F32, name="warm")
+        nc.vector.memset(warm[:, 0:1], 1.0)
+        nc.scalar.activation(warm[:, 1:2], warm[:, 0:1], ACT.Abs_reciprocal_sqrt, bias=ROOT_SHIFT, scale=ROOT_SHIFT)
+
+        def load_rows(rows, raw):
             for half in range(2):
                 cols = slice(half * PASS // 2, (half + 1) * PASS // 2)
                 nc.sync.dma_start(raw[:, half], rows[:, cols].rearrange("(p j) c -> p j c", j=PACK))
             return raw
 
-        def load_vac(b):
-            v = keep.tile([P, PACK, M], F32, name=f"vac{b}", tag=("tab_then_vac", "raw_weights")[b], align_bytes=64)
+        def load_vac(b, v):
             nc.sync.dma_start(v[:], vac[b * PASS : (b + 1) * PASS, :].rearrange("(p j) m -> p j m", j=PACK))
             return v
 
         nc.sync.dma_start(idx1[:], offs)
         nc.sync.dma_start(w2_raw[:].bitcast(I32), w2_words[0].bitcast(I32))
+        for q in range(4):
+            nc.scalar.dma_start(tab_s[32 * q : 32 * q + 4, :].bitcast(I32), tab_scales[0, 4 * q : 4 * q + 4, :].bitcast(I32))
         nc.sync.dma_start(idx2[:], offs2)
         nc.sync.dma_start(idx3[:], offs3)
         nc.sync.dma_start(tab_w[:], tab_words[0].rearrange("p t i -> p (t i)").bitcast(I32))
-        for q in range(4):
-            nc.scalar.dma_start(tab_s[32 * q : 32 * q + 4, :].bitcast(I32), tab_scales[0, 4 * q : 4 * q + 4, :].bitcast(I32))
-        for q in range(4):
-            nc.scalar.dma_start(
-                w2_raw_s[32 * q : 32 * q + 4, :].bitcast(I32), w2_scales[0, 4 * q : 4 * q + 4, :].bitcast(I32)
-            )
-        nc.gpsimd.dma_start(b1_sb[:], b1.rearrange("(b p t) -> p b t", p=P, t=PACK))
-        nc.gpsimd.dma_start(b3_sb[:], b3.rearrange("(p t) -> p t", t=PACK))
 
-        w2_codes = keep.tile([P, 2 * H], U8, name="w2_codes", align_bytes=64)
+        w2_codes = keep.tile([P, 2 * H], U8, name="w2_codes", tag="w2_then_vac", align_bytes=64)
         w2_s = keep.tile([P, H], U8, name="w2_s", align_bytes=64)
         w1_codes = keep.tile([P, H], U32, name="w1_codes", align_bytes=64)
         w1_s = keep.tile([P, H], U8, name="w1_s", align_bytes=64)
@@ -113,7 +108,19 @@ def tile_list_well_vacuum_scores_kernel(
             w2_codes[:].bitcast(U16).rearrange("p (b t m) -> p b t m", b=BLOCKS, t=PACK),
             w2_raw[:].bitcast(U16).rearrange("p (b m t) -> p b t m", b=BLOCKS, t=PACK),
         )
-        w1_raw = load_rows(w1[:, 0:PASS])
+        raw_shape = [P, 2, PACK, PASS // 2]
+        w1_raw = load_rows(w1[:, 0:PASS], head.tile(raw_shape, F32, name="w1_raw0", offset=B1_AT - 8192))
+        wgs_sb = head.tile([P, S], F32, name="wgs_sb", offset=WGS_AT)
+        nc.sync.dma_start(wgs_sb[:], wgs)
+        b1_sb = head.tile([P, BLOCKS, PACK], F32, name="b1_sb", offset=B1_AT)
+        nc.sync.dma_start(b1_sb[:], b1.rearrange("(b p t) -> p b t", p=P, t=PACK))
+        nc.vector.memset(pages[1][:], 0.0)
+        w2_raw_s = head.tile([P, H], U8, name="w2_raw_s", offset=W2S_AT)
+        nc.vector.memset(w2_raw_s[:].bitcast(I32), 0)
+        for q in range(4):
+            nc.scalar.dma_start(
+                w2_raw_s[32 * q : 32 * q + 4, :].bitcast(I32), w2_scales[0, 4 * q : 4 * q + 4, :].bitcast(I32)
+            )
         nc.vector.tensor_copy(v_s[:], tab_s[:].indirect(idx1[:]))
         v_codes = keep.tile([P, S], U32, name="v_codes", tag="scales_then_codes", align_bytes=64)
         nc.vector.tensor_copy(v_codes[:], tab_w[:].bitcast(U32).indirect(idx1[:]))
@@ -121,15 +128,15 @@ def tile_list_well_vacuum_scores_kernel(
             w2_s[:].rearrange("p (b t m) -> p b t m", b=BLOCKS, t=PACK),
             w2_raw_s[:].rearrange("p (b m t) -> p b t m", b=BLOCKS, t=PACK),
         )
-        wgs_sb = keep.tile([P, S], F32, name="wgs_sb", tag="scales_then_wgs", align_bytes=64)
-        nc.sync.dma_start(wgs_sb[:], wgs)
+        b3_sb = head.tile([P, PACK], F32, name="b3_sb", offset=W2S_AT)
+        nc.sync.dma_start(b3_sb[:], b3.rearrange("(p t) -> p t", t=PACK))
         first = keep.tile([P, 2 * PASS], BF16, name="first", tag="grouped_then_wgt", align_bytes=64)
         quantize_weight_pair(w1_raw, 0, w1_codes, w1_s, 0, first)
         wgt_sb = keep.tile([P, M], F32, name="wgt_sb", tag="grouped_then_wgt", align_bytes=64)
         nc.sync.dma_start(wgt_sb[:], wgt)
         quantize_weight_pair(w1_raw, 1, w1_codes, w1_s, 0)
-        w1_raw = load_rows(w1[:, PASS : 2 * PASS])
-        vac_sb = [load_vac(0)]
+        w1_raw = load_rows(w1[:, PASS : 2 * PASS], head.tile(raw_shape, F32, name="w1_raw1", offset=B1_AT - 8192))
+        vac_sb = []
 
         damp = [keep.tile([P, PACK * M], F32, name=f"damp{b}") for b in range(BLOCKS)]
         z_codes = [keep.tile([P, M], U32, name=f"z_codes{b}", align_bytes=64) for b in range(BLOCKS)]
@@ -138,13 +145,13 @@ def tile_list_well_vacuum_scores_kernel(
         x_tiles = {}
 
         last = SLICES - 1
-        work = {-2: ring.tile([P, 2, S], F32, name="work", bufs=3)}
+        work = {-2: ring.tile([P, 2 * S], F32, name="work", bufs=3)}
 
         def products(s):
             cols = slice(s * P, (s + 1) * P)
-            work[s - 1] = ring.tile([P, 2, S], F32, name="work", bufs=3)
-            h = work[s - 1][:, 0, :]
-            valve_sb = work[s - 2][:, 1, :]
+            work[s - 1] = ring.tile([P, 2 * S], F32, name="work", bufs=3)
+            h = work[s - 1][:, 0:S]
+            valve_sb = work[s - 2][:, S : 2 * S]
             for half in range(S // BANK):
                 span = slice(half * BANK, (half + 1) * BANK)
                 valve = psum.tile([P, BANK], F32, name=f"bank{4 * (s % 2) + 2 * half}")
@@ -204,44 +211,39 @@ def tile_list_well_vacuum_scores_kernel(
             return damp[s // PACK][:, at : at + width]
 
         def weigh_taken(s):
-            x = work[s][:, :, 0:BANK]
-            nc.gpsimd.tensor_tensor(
-                x, x_tiles[s][:].rearrange("p (h c) -> p h c", h=2), wgt_sb[:].rearrange("p (h c) -> p h c", h=2), MULT
-            )
+            nc.gpsimd.tensor_tensor(work[s][:, S // 2 : S // 2 + M], x_tiles[s][:], wgt_sb[:], MULT)
 
         def damp_taken(s):
-            x = work[s][:, :, 0:BANK]
-            if s < PACK:
-                pieces = [(damp_piece(s, 0, M).rearrange("p (h c) -> p h c", h=2), x)]
-            else:
-                pieces = [
-                    (damp_piece(s, c0, cw), work[s][:, c0 // BANK, c0 % BANK : c0 % BANK + cw]) for c0, cw in CHUNKS
-                ]
-            damping(s, x, pieces)
-
-        z_rows = keep.tile([P, PACK, M], BF16, name="z_rows", align_bytes=64)
+            x = work[s][:, S // 2 : S // 2 + M]
+            spans = CHUNKS if s >= PACK else [(0, M)]
+            damping(s, x, [(damp_piece(s, c0, cw), x[:, c0 : c0 + cw]) for c0, cw in spans])
 
         def first_z_row(t):
-            nc.gpsimd.tensor_tensor(z_rows[:, t, :], damp[0][:, t * M : (t + 1) * M], vac_sb[0][:, t, :], MULT)
+            row = damp[0][:, t * M : (t + 1) * M]
+            nc.gpsimd.tensor_tensor(row, row, vac_sb[0][:, t, :], MULT)
 
         def quantize_first_z():
+            rows = damp[0][:].rearrange("p (t m) -> p t m", t=PACK)
             for half in range(2):
                 span = slice(half * BANK, (half + 1) * BANK)
                 z = ring.tile([P, PACK * BANK], BF16, name="w_grouped", align_bytes=64)
                 nc.scalar.copy(
-                    z[:].rearrange("p (c i t) -> p c t i", i=4, t=PACK),
-                    z_rows[:, :, span].rearrange("p t (c i) -> p c t i", i=4),
+                    z[:].rearrange("p (c i t) -> p c t i", i=2, t=PACK),
+                    rows[:, :, span].rearrange("p t (c i) -> p c t i", i=2),
                 )
                 nc.vector.quantize_mx(z_codes[0][:, span].bitcast(FP8X4), z_s[0][:, span], z[:])
 
-        def quantize_z(b, start, width):
-            z = ring.tile([P, PACK * 256], BF16, name="z", align_bytes=64)
+        def group_z(b, start, width):
+            z = ring.tile([P, PACK * 256], BF16, name="z", align_bytes=64, bufs=3)
             nc.vector.tensor_tensor(
                 z[:, 0 : PACK * width].rearrange("p (c i t) -> p c t i", i=2, t=PACK),
                 damp[b][:, PACK * start : PACK * (start + width)].rearrange("p (t c i) -> p c t i", t=PACK, i=2),
                 vac_sb[b][:, :, start : start + width].rearrange("p t (c i) -> p c t i", i=2),
                 MULT,
             )
+            return z
+
+        def quantize_z(b, start, width, z):
             span = slice(start, start + width)
             nc.vector.quantize_mx(z_codes[b][:, span].bitcast(FP8X4), z_s[b][:, span], z[:, 0 : PACK * width])
 
@@ -267,12 +269,16 @@ def tile_list_well_vacuum_scores_kernel(
         def store(start, width):
             per_bank = BANK // width
             staged = keep.tile([P, PACK, width], F32, name=f"staged{start}")
-            for t in range(PACK):
-                bank_no = (PACK * start) // BANK + t // per_bank
-                at = (t % per_bank) * width
-                nc.scalar.activation(
-                    staged[:, t, :], score_banks[bank_no][:, at : at + width], ACT.Identity, bias=b3_sb[:, t : t + 1]
-                )
+            if start + width == M:
+                bank = score_banks[(PACK * start) // BANK][:].rearrange("p (t c) -> p t c", t=PACK)
+                nc.vector.tensor_tensor(staged[:], bank, b3_sb[:].unsqueeze(2).to_broadcast([P, PACK, width]), ADD)
+            else:
+                for t in range(PACK):
+                    bank_no = (PACK * start) // BANK + t // per_bank
+                    at = (t % per_bank) * width
+                    nc.scalar.activation(
+                        staged[:, t, :], score_banks[bank_no][:, at : at + width], ACT.Identity, bias=b3_sb[:, t : t + 1]
+                    )
             nc.sync.dma_start(out_rows[:, :, start : start + width], staged[:])
 
         products(0)
@@ -292,15 +298,20 @@ def tile_list_well_vacuum_scores_kernel(
                 take(s)
             if s == 0:
                 quantize_weight_block(w1_raw, w1_codes, w1_s, PASS)
+                vac_sb.append(load_vac(0, head.tile([P, PACK, M], F32, name="vac0", offset=0)))
+            if s == 1:
+                w3_raw = keep.tile([P, BLOCKS] + raw_shape[1:], F32, name="w3_raw", tag="table_then_w3", align_bytes=64)
+                for b in range(BLOCKS):
+                    load_rows(w3[b * PASS : (b + 1) * PASS, :], w3_raw[:, b])
+            if s in (2, 3):
+                quantize_weight_block(w3_raw[:, s - 2], w3_codes, w3_s, (s - 2) * N)
             if s in (4, 5):
                 first_z_row(s - 4)
-                b = s - 4
-                w3_raw = load_rows(w3[b * PASS : (b + 1) * PASS, :])
-                quantize_weight_block(w3_raw, w3_codes, w3_s, b * N)
+            if s == 5:
+                vac_sb.append(load_vac(1, keep.tile([P, PACK, M], F32, name="vac1", tag="w2_then_vac", align_bytes=64)))
             if s == 6:
                 first_z_row(2)
                 first_z_row(3)
-                vac_sb.append(load_vac(1))
                 quantize_first_z()
         for start, width in CHUNKS:
             scores(0, start, width)
@@ -309,7 +320,10 @@ def tile_list_well_vacuum_scores_kernel(
             take_weighed(last, start, width)
             x = x_tiles[last][:, start : start + width]
             damping(last, x, [(damp_piece(last, start, width), x)])
-        for start, width in CHUNKS:
-            quantize_z(1, start, width)
+        grouped_z = [group_z(1, *CHUNKS[0])]
+        for c, (start, width) in enumerate(CHUNKS):
+            if c + 1 < len(CHUNKS):
+                grouped_z.append(group_z(1, *CHUNKS[c + 1]))
+            quantize_z(1, start, width, grouped_z[c])
             scores(1, start, width)
             store(start, width)

@@ -27,8 +27,7 @@ SLICES = BLOCKS * PACK
 CHUNKS = [(0, 256), (256, 256), (512, 256), (768, 128), (896, 128)]
 ROOT_SHIFT = 1.125
 B1_AT = 16384
-W2S_AT = B1_AT + 32
-WGS_AT = W2S_AT + H
+TAB_AT = B1_AT + 64
 
 
 def tile_list_well_vacuum_scores_kernel(
@@ -44,12 +43,13 @@ def tile_list_well_vacuum_scores_kernel(
         idx1 = keep.tile([P, S // 16], U16, name="idx1")
         idx2 = keep.tile([P, S // 16], U16, name="idx2")
         idx3 = keep.tile([P, M // 16], U16, name="idx3")
-        tab_w = keep.tile([P, T], I32, name="tab_w", tag="table_then_w3", align_bytes=64)
+        w2_raw_s = keep.tile([P, H], U8, name="w2_raw_s", tag="scales_then_b3", align_bytes=64)
         tab_s = keep.tile([P, T], U8, name="tab_s", tag="scales_then_codes", align_bytes=64)
         w2_raw = head.tile([P, 2 * H], U8, name="w2_raw", offset=B1_AT - 512)
         pages = [keep.tile([P, T2], F32, name=f"page{i}") for i in range(2)]
 
         nc.vector.memset(tab_s[:].bitcast(I32), 0)
+        nc.vector.memset(w2_raw_s[:].bitcast(I32), 0)
         nc.vector.memset(pages[0][:], 0.0)
 
         warm = keep.tile([P, 2], F32, name="warm")
@@ -66,13 +66,13 @@ def tile_list_well_vacuum_scores_kernel(
             nc.sync.dma_start(v[:], vac[b * PASS : (b + 1) * PASS, :].rearrange("(p j) m -> p j m", j=PACK))
             return v
 
-        nc.sync.dma_start(idx1[:], offs)
         nc.sync.dma_start(w2_raw[:].bitcast(I32), w2_words[0].bitcast(I32))
-        for q in range(4):
-            nc.scalar.dma_start(tab_s[32 * q : 32 * q + 4, :].bitcast(I32), tab_scales[0, 4 * q : 4 * q + 4, :].bitcast(I32))
+        nc.sync.dma_start(idx1[:], offs)
         nc.sync.dma_start(idx2[:], offs2)
         nc.sync.dma_start(idx3[:], offs3)
-        nc.sync.dma_start(tab_w[:], tab_words[0].rearrange("p t i -> p (t i)").bitcast(I32))
+        for plane, rows in ((tab_s, tab_scales), (w2_raw_s, w2_scales)):
+            for q in range(4):
+                nc.sync.dma_start(plane[32 * q : 32 * q + 4, :].bitcast(I32), rows[0, 4 * q : 4 * q + 4, :].bitcast(I32))
 
         w2_codes = keep.tile([P, 2 * H], U8, name="w2_codes", tag="w2_then_vac", align_bytes=64)
         w2_s = keep.tile([P, H], U8, name="w2_s", align_bytes=64)
@@ -108,28 +108,24 @@ def tile_list_well_vacuum_scores_kernel(
             w2_codes[:].bitcast(U16).rearrange("p (b t m) -> p b t m", b=BLOCKS, t=PACK),
             w2_raw[:].bitcast(U16).rearrange("p (b m t) -> p b t m", b=BLOCKS, t=PACK),
         )
+        tab_w = head.tile([P, T], I32, name="tab_w", offset=TAB_AT)
+        nc.sync.dma_start(tab_w[:], tab_words[0].rearrange("p t i -> p (t i)").bitcast(I32))
         raw_shape = [P, 2, PACK, PASS // 2]
         w1_raw = load_rows(w1[:, 0:PASS], head.tile(raw_shape, F32, name="w1_raw0", offset=B1_AT - 8192))
-        wgs_sb = head.tile([P, S], F32, name="wgs_sb", offset=WGS_AT)
-        nc.sync.dma_start(wgs_sb[:], wgs)
         b1_sb = head.tile([P, BLOCKS, PACK], F32, name="b1_sb", offset=B1_AT)
         nc.sync.dma_start(b1_sb[:], b1.rearrange("(b p t) -> p b t", p=P, t=PACK))
+        b3_sb = head.tile([P, PACK], F32, name="b3_sb", offset=B1_AT + 32)
+        nc.sync.dma_start(b3_sb[:], b3.rearrange("(p t) -> p t", t=PACK))
         nc.vector.memset(pages[1][:], 0.0)
-        w2_raw_s = head.tile([P, H], U8, name="w2_raw_s", offset=W2S_AT)
-        nc.vector.memset(w2_raw_s[:].bitcast(I32), 0)
-        for q in range(4):
-            nc.scalar.dma_start(
-                w2_raw_s[32 * q : 32 * q + 4, :].bitcast(I32), w2_scales[0, 4 * q : 4 * q + 4, :].bitcast(I32)
-            )
-        nc.vector.tensor_copy(v_s[:], tab_s[:].indirect(idx1[:]))
-        v_codes = keep.tile([P, S], U32, name="v_codes", tag="scales_then_codes", align_bytes=64)
-        nc.vector.tensor_copy(v_codes[:], tab_w[:].bitcast(U32).indirect(idx1[:]))
         nc.vector.tensor_copy(
             w2_s[:].rearrange("p (b t m) -> p b t m", b=BLOCKS, t=PACK),
             w2_raw_s[:].rearrange("p (b m t) -> p b t m", b=BLOCKS, t=PACK),
         )
-        b3_sb = head.tile([P, PACK], F32, name="b3_sb", offset=W2S_AT)
-        nc.sync.dma_start(b3_sb[:], b3.rearrange("(p t) -> p t", t=PACK))
+        nc.vector.tensor_copy(v_s[:], tab_s[:].indirect(idx1[:]))
+        v_codes = keep.tile([P, S], U32, name="v_codes", tag="scales_then_codes", align_bytes=64)
+        nc.vector.tensor_copy(v_codes[:], tab_w[:].bitcast(U32).indirect(idx1[:]))
+        wgs_sb = keep.tile([P, S], F32, name="wgs_sb", tag="scales_then_b3", align_bytes=64)
+        nc.sync.dma_start(wgs_sb[:], wgs)
         first = keep.tile([P, 2 * PASS], BF16, name="first", tag="grouped_then_wgt", align_bytes=64)
         quantize_weight_pair(w1_raw, 0, w1_codes, w1_s, 0, first)
         wgt_sb = keep.tile([P, M], F32, name="wgt_sb", tag="grouped_then_wgt", align_bytes=64)
@@ -300,7 +296,7 @@ def tile_list_well_vacuum_scores_kernel(
                 quantize_weight_block(w1_raw, w1_codes, w1_s, PASS)
                 vac_sb.append(load_vac(0, head.tile([P, PACK, M], F32, name="vac0", offset=0)))
             if s == 1:
-                w3_raw = keep.tile([P, BLOCKS] + raw_shape[1:], F32, name="w3_raw", tag="table_then_w3", align_bytes=64)
+                w3_raw = head.tile([P, BLOCKS] + raw_shape[1:], F32, name="w3_raw", offset=TAB_AT)
                 for b in range(BLOCKS):
                     load_rows(w3[b * PASS : (b + 1) * PASS, :], w3_raw[:, b])
             if s in (2, 3):

import math
from contextlib import ExitStack

import concourse.mybir as mybir

K, T, S, H, T2, M, N = 512, 4096, 1024, 1024, 2048, 1024, 512
FLOPS = 2 * (2 * K * H * S + H * N * M)

F32 = mybir.dt.float32
BF16 = mybir.dt.bfloat16
I32 = mybir.dt.int32
U32 = mybir.dt.uint32
U16 = mybir.dt.uint16
U8 = mybir.dt.uint8
FP8X4 = mybir.dt.float8_e4m3fn_x4
FP4X4 = mybir.dt.float4_e2m1fn_x4
ACT = mybir.ActivationFunctionType
MULT = mybir.AluOpType.mult
ADD = mybir.AluOpType.add

P = 128
PACK = 4
PASS = P * PACK
BANK = 512
BLOCKS = H // PASS
SLICES = BLOCKS * PACK
CHUNKS = [(0, 256), (256, 256), (512, 256), (768, 128), (896, 128)]
ROOT_SHIFT = 1.125
B1_AT = 16384
TAB_AT = B1_AT + 64


def tile_list_well_vacuum_scores_kernel(
    tc, tab_words, tab_scales, offs, offs2, offs3, w1, w2_words, w2_scales, b1, wgs, wgt, vac, w3, b3, out
):
    nc = tc.nc
    with ExitStack() as ctx:
        keep = ctx.enter_context(tc.tile_pool(name="keep", bufs=1))
        ring = ctx.enter_context(tc.tile_pool(name="ring", bufs=2))
        head = ctx.enter_context(tc.tile_pool(name="head", bufs=1))
        psum = ctx.enter_context(tc.psum_pool(name="psum", bufs=1))

        idx1 = keep.tile([P, S // 16], U16, name="idx1")
        idx2 = keep.tile([P, S // 16], U16, name="idx2")
        idx3 = keep.tile([P, M // 16], U16, name="idx3")
        w2_raw_s = keep.tile([P, H], U8, name="w2_raw_s", tag="scales_then_b3", align_bytes=64)
        tab_s = keep.tile([P, T], U8, name="tab_s", tag="scales_then_codes", align_bytes=64)
        w2_raw = head.tile([P, 2 * H], U8, name="w2_raw", offset=B1_AT - 512)
        pages = [keep.tile([P, T2], F32, name=f"page{i}") for i in range(2)]

        nc.vector.memset(tab_s[:].bitcast(I32), 0)
        nc.vector.memset(w2_raw_s[:].bitcast(I32), 0)
        nc.vector.memset(pages[0][:], 0.0)

        warm = keep.tile([P, 2], F32, name="warm")
        nc.vector.memset(warm[:, 0:1], 1.0)
        nc.scalar.activation(warm[:, 1:2], warm[:, 0:1], ACT.Abs_reciprocal_sqrt, bias=ROOT_SHIFT, scale=ROOT_SHIFT)

        def load_rows(rows, raw):
            for half in range(2):
                cols = slice(half * PASS // 2, (half + 1) * PASS // 2)
                nc.sync.dma_start(raw[:, half], rows[:, cols].rearrange("(p j) c -> p j c", j=PACK))
            return raw

        def load_vac(b, v):
            nc.sync.dma_start(v[:], vac[b * PASS : (b + 1) * PASS, :].rearrange("(p j) m -> p j m", j=PACK))
            return v

        nc.sync.dma_start(w2_raw[:].bitcast(I32), w2_words[0].bitcast(I32))
        nc.sync.dma_start(idx1[:], offs)
        nc.sync.dma_start(idx2[:], offs2)
        nc.sync.dma_start(idx3[:], offs3)
        for plane, rows in ((tab_s, tab_scales), (w2_raw_s, w2_scales)):
            for q in range(4):
                nc.sync.dma_start(plane[32 * q : 32 * q + 4, :].bitcast(I32), rows[0, 4 * q : 4 * q + 4, :].bitcast(I32))

        w2_codes = keep.tile([P, 2 * H], U8, name="w2_codes", tag="w2_then_vac", align_bytes=64)
        w2_s = keep.tile([P, H], U8, name="w2_s", align_bytes=64)
        w1_codes = keep.tile([P, H], U32, name="w1_codes", align_bytes=64)
        w1_s = keep.tile([P, H], U8, name="w1_s", align_bytes=64)
        w3_codes = keep.tile([P, BLOCKS * N], U32, name="w3_codes", align_bytes=64)
        w3_s = keep.tile([P, BLOCKS * N], U8, name="w3_s", align_bytes=64)

        def quantize_weight_pair(raw, pair, codes, scales, col0, grouped=None):
            if grouped is None:
                grouped = ring.tile([P, 2 * PASS], BF16, name="w_grouped", align_bytes=64)
            for half in range(2):
                nc.scalar.copy(
                    grouped[:].rearrange("p (t h m j) -> p h m j t", t=2, h=2, j=PACK)[:, half],
                    raw[:, half].rearrange("p j (m t) -> p m j t", t=PACK)[:, :, :, 2 * pair : 2 * pair + 2],
                )
            cols = slice(col0 + 2 * P * pair, col0 + 2 * P * (pair + 1))
            nc.vector.quantize_mx(codes[:, cols].bitcast(FP8X4), scales[:, cols], grouped[:])

        def quantize_weight_block(raw, codes, scales, col0):
            grouped = ring.tile([P, PACK * PASS], BF16, name="w_grouped", align_bytes=64)
            for pair in range(2):
                for half in range(2):
                    nc.scalar.copy(
                        grouped[:].rearrange("p (u t h m j) -> p u h m j t", u=2, t=2, h=2, j=PACK)[:, pair, half],
                        raw[:, half].rearrange("p j (m t) -> p m j t", t=PACK)[:, :, :, 2 * pair : 2 * pair + 2],
                    )
            cols = slice(col0, col0 + PASS)
            nc.vector.quantize_mx(codes[:, cols].bitcast(FP8X4), scales[:, cols], grouped[:])

        v_s = keep.tile([P, S], U8, name="v_s", align_bytes=64)
        nc.vector.tensor_copy(
            w2_codes[:].bitcast(U16).rearrange("p (b t m) -> p b t m", b=BLOCKS, t=PACK),
            w2_raw[:].bitcast(U16).rearrange("p (b m t) -> p b t m", b=BLOCKS, t=PACK),
        )
        tab_w = head.tile([P, T], I32, name="tab_w", offset=TAB_AT)
        nc.sync.dma_start(tab_w[:], tab_words[0].rearrange("p t i -> p (t i)").bitcast(I32))
        raw_shape = [P, 2, PACK, PASS // 2]
        w1_raw = load_rows(w1[:, 0:PASS], head.tile(raw_shape, F32, name="w1_raw0", offset=B1_AT - 8192))
        b1_sb = head.tile([P, BLOCKS, PACK], F32, name="b1_sb", offset=B1_AT)
        nc.sync.dma_start(b1_sb[:], b1.rearrange("(b p t) -> p b t", p=P, t=PACK))
        b3_sb = head.tile([P, PACK], F32, name="b3_sb", offset=B1_AT + 32)
        nc.sync.dma_start(b3_sb[:], b3.rearrange("(p t) -> p t", t=PACK))
        nc.vector.memset(pages[1][:], 0.0)
        nc.vector.tensor_copy(
            w2_s[:].rearrange("p (b t m) -> p b t m", b=BLOCKS, t=PACK),
            w2_raw_s[:].rearrange("p (b m t) -> p b t m", b=BLOCKS, t=PACK),
        )
        nc.vector.tensor_copy(v_s[:], tab_s[:].indirect(idx1[:]))
        v_codes = keep.tile([P, S], U32, name="v_codes", tag="scales_then_codes", align_bytes=64)
        nc.vector.tensor_copy(v_codes[:], tab_w[:].bitcast(U32).indirect(idx1[:]))
        wgs_sb = keep.tile([P, S], F32, name="wgs_sb", tag="scales_then_b3", align_bytes=64)
        nc.sync.dma_start(wgs_sb[:], wgs)
        first = keep.tile([P, 2 * PASS], BF16, name="first", tag="grouped_then_wgt", align_bytes=64)
        quantize_weight_pair(w1_raw, 0, w1_codes, w1_s, 0, first)
        wgt_sb = keep.tile([P, M], F32, name="wgt_sb", tag="grouped_then_wgt", align_bytes=64)
        nc.sync.dma_start(wgt_sb[:], wgt)
        quantize_weight_pair(w1_raw, 1, w1_codes, w1_s, 0)
        w1_raw = load_rows(w1[:, PASS : 2 * PASS], head.tile(raw_shape, F32, name="w1_raw1", offset=B1_AT - 8192))
        vac_sb = []

        damp = [keep.tile([P, PACK * M], F32, name=f"damp{b}") for b in range(BLOCKS)]
        z_codes = [keep.tile([P, M], U32, name=f"z_codes{b}", align_bytes=64) for b in range(BLOCKS)]
        z_s = [keep.tile([P, M], U8, name=f"z_s{b}", align_bytes=64) for b in range(BLOCKS)]
        h_tiles = {}
        x_tiles = {}

        last = SLICES - 1
        work = {-2: ring.tile([P, 2 * S], F32, name="work", bufs=3)}

        def products(s):
            cols = slice(s * P, (s + 1) * P)
            work[s - 1] = ring.tile([P, 2 * S], F32, name="work", bufs=3)
            h = work[s - 1][:, 0:S]
            valve_sb = work[s - 2][:, S : 2 * S]
            for half in range(S // BANK):
                span = slice(half * BANK, (half + 1) * BANK)
                valve = psum.tile([P, BANK], F32, name=f"bank{4 * (s % 2) + 2 * half}")
                flow = psum.tile([P, BANK], F32, name=f"bank{4 * (s % 2) + 2 * half + 1}")
                nc.tensor.matmul_mx(
                    valve[:], w2_codes[:, 2 * s * P : 2 * (s + 1) * P].bitcast(FP4X4), w2_s[:, cols],
                    v_codes[:, span].bitcast(FP8X4), v_s[:, span], start=True, stop=True,
                )
                nc.tensor.matmul_mx(
                    flow[:], w1_codes[:, cols].bitcast(FP8X4), w1_s[:, cols],
                    v_codes[:, span].bitcast(FP8X4), v_s[:, span], start=True, stop=True,
                )
                nc.scalar.copy(valve_sb[:, span], valve[:])
                if s == 0:
                    nc.vector.tensor_tensor(h[:, span], flow[:], valve_sb[:, span], MULT)
                else:
                    nc.scalar.copy(h[:, span], flow[:])
            if s > 0:
                nc.gpsimd.tensor_tensor(h, h, valve_sb, MULT)
            h_tiles[s] = h

        def weigh(s):
            h = h_tiles[s]
            bias = b1_sb[:, s // PACK, s % PACK : s % PACK + 1]
            if s == 0:
                for half in range(S // BANK):
                    span = slice(half * BANK, (half + 1) * BANK)
                    nc.vector.scalar_tensor_tensor(h[:, span], h[:, span], bias, wgs_sb[:, span], ADD, MULT)
            else:
                nc.scalar.activation(h, h, ACT.Identity, bias=bias)
                placed = ring.tile([P, S], F32, name="placed")
                nc.gpsimd.tensor_tensor(placed[:], h, wgs_sb[:], MULT)
                h_tiles[s] = placed[:]

        def put(s):
            nc.vector.tensor_copy(pages[s % 2][:].indirect(idx2[:]), h_tiles[s])

        def take(s):
            x_tiles[s] = ring.tile([P, M], F32, name="x")
            nc.vector.tensor_copy(x_tiles[s][:], pages[s % 2][:].indirect(idx3[:]))

        def take_weighed(s, start, width):
            span = slice(start, start + width)
            nc.vector.tensor_tensor(
                x_tiles[s][:, span], pages[s % 2][:].indirect(idx3[:, start // 16 : (start + width) // 16]),
                wgt_sb[:, span], MULT,
            )

        def damping(s, x, pieces):
            nc.scalar.activation(x, x, ACT.Square)
            nc.scalar.activation(x, x, ACT.Abs_reciprocal_sqrt, bias=ROOT_SHIFT, scale=ROOT_SHIFT)
            for dst, src in pieces:
                nc.scalar.activation(dst, src, ACT.Square, scale=math.sqrt(ROOT_SHIFT))

        def damp_piece(s, start, width):
            at = PACK * start + (s % PACK) * width
            return damp[s // PACK][:, at : at + width]

        def weigh_taken(s):
            nc.gpsimd.tensor_tensor(work[s][:, S // 2 : S // 2 + M], x_tiles[s][:], wgt_sb[:], MULT)

        def damp_taken(s):
            x = work[s][:, S // 2 : S // 2 + M]
            spans = CHUNKS if s >= PACK else [(0, M)]
            damping(s, x, [(damp_piece(s, c0, cw), x[:, c0 : c0 + cw]) for c0, cw in spans])

        def first_z_row(t):
            row = damp[0][:, t * M : (t + 1) * M]
            nc.gpsimd.tensor_tensor(row, row, vac_sb[0][:, t, :], MULT)

        def quantize_first_z():
            rows = damp[0][:].rearrange("p (t m) -> p t m", t=PACK)
            for half in range(2):
                span = slice(half * BANK, (half + 1) * BANK)
                z = ring.tile([P, PACK * BANK], BF16, name="w_grouped", align_bytes=64)
                nc.scalar.copy(
                    z[:].rearrange("p (c i t) -> p c t i", i=2, t=PACK),
                    rows[:, :, span].rearrange("p t (c i) -> p c t i", i=2),
                )
                nc.vector.quantize_mx(z_codes[0][:, span].bitcast(FP8X4), z_s[0][:, span], z[:])

        def group_z(b, start, width):
            z = ring.tile([P, PACK * 256], BF16, name="z", align_bytes=64, bufs=3)
            nc.vector.tensor_tensor(
                z[:, 0 : PACK * width].rearrange("p (c i t) -> p c t i", i=2, t=PACK),
                damp[b][:, PACK * start : PACK * (start + width)].rearrange("p (t c i) -> p c t i", t=PACK, i=2),
                vac_sb[b][:, :, start : start + width].rearrange("p t (c i) -> p c t i", i=2),
                MULT,
            )
            return z

        def quantize_z(b, start, width, z):
            span = slice(start, start + width)
            nc.vector.quantize_mx(z_codes[b][:, span].bitcast(FP8X4), z_s[b][:, span], z[:, 0 : PACK * width])

        score_banks = {}

        def scores(b, start, width):
            per_bank = BANK // width
            span = slice(start, start + width)
            for t in range(PACK):
                bank_no = (PACK * start) // BANK + t // per_bank
                if bank_no not in score_banks:
                    score_banks[bank_no] = psum.tile([P, BANK], F32, name=f"bank{bank_no}")
                at = (t % per_bank) * width
                cols = slice(b * N + t * P, b * N + (t + 1) * P)
                nc.tensor.matmul_mx(
                    score_banks[bank_no][:, at : at + width], w3_codes[:, cols].bitcast(FP8X4), w3_s[:, cols],
                    z_codes[b][:, span].bitcast(FP8X4), z_s[b][:, span],
                    start=(b == 0 and t % per_bank == 0), stop=(b == BLOCKS - 1 and t % per_bank == per_bank - 1),
                )

        out_rows = out.rearrange("(p t) m -> p t m", t=PACK)

        def store(start, width):
            per_bank = BANK // width
            staged = keep.tile([P, PACK, width], F32, name=f"staged{start}")
            if start + width == M:
                bank = score_banks[(PACK * start) // BANK][:].rearrange("p (t c) -> p t c", t=PACK)
                nc.vector.tensor_tensor(staged[:], bank, b3_sb[:].unsqueeze(2).to_broadcast([P, PACK, width]), ADD)
            else:
                for t in range(PACK):
                    bank_no = (PACK * start) // BANK + t // per_bank
                    at = (t % per_bank) * width
                    nc.scalar.activation(
                        staged[:, t, :], score_banks[bank_no][:, at : at + width], ACT.Identity, bias=b3_sb[:, t : t + 1]
                    )
            nc.sync.dma_start(out_rows[:, :, start : start + width], staged[:])

        products(0)
        weigh(0)
        products(1)
        for s in range(SLICES):
            put(s)
            if s >= 1:
                weigh_taken(s - 1)
            if s + 1 <= last:
                weigh(s + 1)
            if s + 2 <= last:
                products(s + 2)
            if s >= 1:
                damp_taken(s - 1)
            if s < last:
                take(s)
            if s == 0:
                quantize_weight_block(w1_raw, w1_codes, w1_s, PASS)
                vac_sb.append(load_vac(0, head.tile([P, PACK, M], F32, name="vac0", offset=0)))
            if s == 1:
                w3_raw = head.tile([P, BLOCKS] + raw_shape[1:], F32, name="w3_raw", offset=TAB_AT)
                for b in range(BLOCKS):
                    load_rows(w3[b * PASS : (b + 1) * PASS, :], w3_raw[:, b])
            if s in (2, 3):
                quantize_weight_block(w3_raw[:, s - 2], w3_codes, w3_s, (s - 2) * N)
            if s in (4, 5):
                first_z_row(s - 4)
            if s == 5:
                vac_sb.append(load_vac(1, keep.tile([P, PACK, M], F32, name="vac1", tag="w2_then_vac", align_bytes=64)))
            if s == 6:
                first_z_row(2)
                first_z_row(3)
                quantize_first_z()
        for start, width in CHUNKS:
            scores(0, start, width)
        x_tiles[last] = ring.tile([P, M], F32, name="x")
        for start, width in CHUNKS:
            take_weighed(last, start, width)
            x = x_tiles[last][:, start : start + width]
            damping(last, x, [(damp_piece(last, start, width), x)])
        grouped_z = [group_z(1, *CHUNKS[0])]
        for c, (start, width) in enumerate(CHUNKS):
            if c + 1 < len(CHUNKS):
                grouped_z.append(group_z(1, *CHUNKS[c + 1]))
            quantize_z(1, start, width, grouped_z[c])
            scores(1, start, width)
            store(start, width)
